import numpy as np
import ml_dtypes


def mxq(x, axis, fmt="e4m3"):
    dtype, down = {"e4m3": (ml_dtypes.float8_e4m3fn, 7), "e5m2": (ml_dtypes.float8_e5m2, 14)}[fmt]
    v = np.moveaxis(np.asarray(x, np.float32).astype(ml_dtypes.bfloat16).astype(np.float64), axis, -1)
    blocks = v.reshape(v.shape[:-1] + (-1, 32))
    amax = np.abs(blocks).max(-1, keepdims=True)
    byte = np.maximum(np.where(amax > 0, np.frexp(amax)[1] - 1 + 127, 0) - down, 1)
    scale = np.exp2(byte - 127.0)
    codes = (blocks / scale).astype(np.float32).astype(dtype).astype(np.float64)
    return np.moveaxis((codes * scale).reshape(v.shape), -1, axis)


WIDE = False


def mx_kscale(k, group=512):
    if not WIDE:
        return np.ones(k)
    levels = np.array([10, -10, 5, -5, 0])
    if group != 512:
        return np.exp2(np.random.permutation(np.resize(levels, k // group))).repeat(group)
    if k % 512:
        return np.exp2(np.random.permutation(np.resize(levels, k // 32))).repeat(32)
    a = np.empty((k // 512, 16))
    for p in range(k // 512):
        a[p, :8] = np.random.permutation(np.resize(levels, 8))
        for g in range(8):
            far = levels[np.abs(levels - a[p, g]) >= 10]
            a[p, g + 8] = far[np.random.randint(len(far))]
    return np.exp2(a.ravel()).repeat(32)


def f64(x):
    return np.asarray(x).astype(np.float64)


G, D, M, N = 2, 256, 256, 512


def setup_inputs():
    n = np.random.standard_normal
    s = mx_kscale(D, 0)[:, None]
    return {
        "x": (n((G, D, N)) * s).astype(np.float32),
        "w": (n((G, D, M)) / np.sqrt(D) / s).astype(np.float32),
        "u": (n((G, D, M)) / np.sqrt(D) / s).astype(np.float32),
    }


def reference(x, w, u):
    xq = mxq(f64(x), 1, "e4m3")
    h = mxq(f64(w), 1, "e4m3").transpose(0, 2, 1) @ xq
    g = mxq(f64(u), 1, "e4m3").transpose(0, 2, 1) @ xq
    y = 1.0 / (1.0 + np.exp(-(h))) * g
    return y

@@ -1,0 +1,108 @@
+from contextlib import ExitStack
+
+import concourse.mybir as mybir
+
+G, D, M, N = 2, 256, 256, 512
+FLOPS = 2 * 2 * G * D * M * N
+
+F32 = mybir.dt.float32
+BF16 = mybir.dt.bfloat16
+U32 = mybir.dt.uint32
+U8 = mybir.dt.uint8
+FP8X4 = mybir.dt.float8_e4m3fn_x4
+SIGMOID = mybir.ActivationFunctionType.Sigmoid
+
+P = 128
+PACK = 4
+ROWS = D // PACK
+M_TILE = 128
+RUN = 4
+X_HALF = N // 2
+X_VECTOR_COLS = 336
+
+
+def interleave(copy, grouped, raw, c0, c1):
+    copy(
+        out=grouped[:, c0 * PACK : c1 * PACK].rearrange("p (c i j) -> p c j i", i=RUN, j=PACK),
+        in_=raw[:, :, c0:c1].rearrange("p j (c i) -> p c j i", i=RUN),
+    )
+
+
+def quantize(nc, codes, scales, grouped, c0, c1):
+    nc.vector.quantize_mx(
+        out=codes[:, c0:c1].bitcast(FP8X4),
+        scales=scales[:, c0:c1],
+        in_=grouped[:, c0 * PACK : c1 * PACK],
+    )
+
+
+def tile_rows_gglu_sigmoid_kernel(tc, x, w, u, out):
+    nc = tc.nc
+    with ExitStack() as ctx:
+        sb = ctx.enter_context(tc.tile_pool(name="sb", bufs=1))
+        ps = ctx.enter_context(tc.psum_pool(name="ps", bufs=1))
+        ctx.enter_context(tc.manual_schedule())
+
+        x_raw = sb.tile([P, PACK, N], F32, name="x_raw", align_bytes=64)
+        w_raw = sb.tile([P, PACK, M], F32, name="w_raw", align_bytes=64)
+        u_raw = sb.tile([P, PACK, M], F32, name="u_raw", align_bytes=64)
+        for raw, src in ((x_raw, x), (w_raw, w), (u_raw, u)):
+            nc.sync.dma_start(out=raw[:], in_=src.rearrange("g (p j) c -> (g p) j c", j=PACK))
+
+        warm_in = sb.tile([P, 1], F32, name="warm_in")
+        warm_out = sb.tile([P, 1], F32, name="warm_out")
+        nc.gpsimd.memset(warm_in[:], 0.0)
+        nc.scalar.activation(out=warm_out[:], in_=warm_in[:], func=SIGMOID)
+
+        x_bf = sb.tile([P, N * PACK], BF16, name="x_bf", align_bytes=64)
+        x_codes = sb.tile([P, N], U32, name="x_codes", align_bytes=64)
+        x_scales = sb.tile([P, N], U8, name="x_scales", align_bytes=64)
+        w_bf = sb.tile([P, M * PACK], BF16, name="w_bf", align_bytes=64)
+        w_codes = sb.tile([P, M], U32, name="w_codes", align_bytes=64)
+        w_scales = sb.tile([P, M], U8, name="w_scales", align_bytes=64)
+        u_bf = sb.tile([P, M * PACK], BF16, name="u_bf", align_bytes=64)
+        u_codes = sb.tile([P, M], U32, name="u_codes", align_bytes=64)
+        u_scales = sb.tile([P, M], U8, name="u_scales", align_bytes=64)
+
+        def product(codes, scales, half, label):
+            banks = []
+            cols = slice(half * M_TILE, (half + 1) * M_TILE)
+            for g in range(G):
+                rows = slice(g * ROWS, (g + 1) * ROWS)
+                bank = ps.tile([M_TILE, N], F32, name="%s_%d_%d" % (label, half, g))
+                nc.tensor.matmul_mx(
+                    out=bank[:],
+                    lhsT=codes[rows, cols].bitcast(FP8X4),
+                    lhsT_scale=scales[rows, cols],
+                    rhs=x_codes[rows, :].bitcast(FP8X4),
+                    rhs_scale=x_scales[rows, :],
+                    start=True,
+                    stop=True,
+                )
+                banks.append(bank)
+            return banks
+
+        interleave(nc.vector.tensor_copy, x_bf, x_raw, 0, X_HALF)
+        interleave(nc.vector.tensor_copy, x_bf, x_raw, X_HALF, X_VECTOR_COLS)
+        interleave(nc.scalar.copy, x_bf, x_raw, X_VECTOR_COLS, N)
+        quantize(nc, x_codes, x_scales, x_bf, 0, X_HALF)
+        quantize(nc, x_codes, x_scales, x_bf, X_HALF, N)
+
+        interleave(nc.scalar.copy, w_bf, w_raw, 0, M_TILE)
+        interleave(nc.vector.tensor_copy, w_bf, w_raw, M_TILE, M)
+        quantize(nc, w_codes, w_scales, w_bf, 0, M_TILE)
+        interleave(nc.vector.tensor_copy, u_bf, u_raw, 0, M_TILE)
+        interleave(nc.scalar.copy, u_bf, u_raw, M_TILE, M)
+        quantize(nc, w_codes, w_scales, w_bf, M_TILE, M)
+        quantize(nc, u_codes, u_scales, u_bf, 0, M_TILE)
+        quantize(nc, u_codes, u_scales, u_bf, M_TILE, M)
+
+        for half in range(M // M_TILE):
+            z_banks = product(w_codes, w_scales, half, "z")
+            v_banks = product(u_codes, u_scales, half, "v")
+            for g in range(G):
+                gate = sb.tile([M_TILE, N], F32, name="gate_%d_%d" % (half, g), align_bytes=64)
+                nc.scalar.activation(out=gate[:], in_=z_banks[g][:], func=SIGMOID)
+                res = sb.tile([M_TILE, N], F32, name="res_%d_%d" % (half, g), align_bytes=64)
+                nc.vector.tensor_tensor(out=res[:], in0=v_banks[g][:], in1=gate[:], op=mybir.AluOpType.mult)
+                nc.sync.dma_start(out=out[g, half * M_TILE : (half + 1) * M_TILE, :], in_=res[:])

@@ -18,7 +18,9 @@ ROWS = D // PACK
 M_TILE = 128
 RUN = 4
 X_HALF = N // 2
-X_VECTOR_COLS = 336
+X_VECTOR_COLS = 288
+W_VECTOR_COLS = 64
+U_VECTOR_COLS = 80
 
 
 def interleave(copy, grouped, raw, c0, c1):
@@ -82,27 +84,35 @@ def tile_rows_gglu_sigmoid_kernel(tc, x, w, u, out):
                 banks.append(bank)
             return banks
 
-        interleave(nc.vector.tensor_copy, x_bf, x_raw, 0, X_HALF)
-        interleave(nc.vector.tensor_copy, x_bf, x_raw, X_HALF, X_VECTOR_COLS)
-        interleave(nc.scalar.copy, x_bf, x_raw, X_VECTOR_COLS, N)
+        vcopy, scopy = nc.vector.tensor_copy, nc.scalar.copy
+        interleave(vcopy, x_bf, x_raw, 0, X_HALF)
+        interleave(vcopy, x_bf, x_raw, X_HALF, X_VECTOR_COLS)
+        interleave(scopy, x_bf, x_raw, X_VECTOR_COLS, N)
         quantize(nc, x_codes, x_scales, x_bf, 0, X_HALF)
+        interleave(vcopy, w_bf, w_raw, 0, W_VECTOR_COLS)
+        interleave(scopy, w_bf, w_raw, W_VECTOR_COLS, M_TILE)
+        interleave(scopy, w_bf, w_raw, M_TILE, M)
         quantize(nc, x_codes, x_scales, x_bf, X_HALF, N)
-
-        interleave(nc.scalar.copy, w_bf, w_raw, 0, M_TILE)
-        interleave(nc.vector.tensor_copy, w_bf, w_raw, M_TILE, M)
         quantize(nc, w_codes, w_scales, w_bf, 0, M_TILE)
-        interleave(nc.vector.tensor_copy, u_bf, u_raw, 0, M_TILE)
-        interleave(nc.scalar.copy, u_bf, u_raw, M_TILE, M)
         quantize(nc, w_codes, w_scales, w_bf, M_TILE, M)
+        for m0 in range(0, M, M_TILE):
+            interleave(vcopy, u_bf, u_raw, m0, m0 + U_VECTOR_COLS)
+            interleave(scopy, u_bf, u_raw, m0 + U_VECTOR_COLS, m0 + M_TILE)
         quantize(nc, u_codes, u_scales, u_bf, 0, M_TILE)
         quantize(nc, u_codes, u_scales, u_bf, M_TILE, M)
 
-        for half in range(M // M_TILE):
-            z_banks = product(w_codes, w_scales, half, "z")
-            v_banks = product(u_codes, u_scales, half, "v")
-            for g in range(G):
-                gate = sb.tile([M_TILE, N], F32, name="gate_%d_%d" % (half, g), align_bytes=64)
-                nc.scalar.activation(out=gate[:], in_=z_banks[g][:], func=SIGMOID)
-                res = sb.tile([M_TILE, N], F32, name="res_%d_%d" % (half, g), align_bytes=64)
-                nc.vector.tensor_tensor(out=res[:], in0=v_banks[g][:], in1=gate[:], op=mybir.AluOpType.mult)
-                nc.sync.dma_start(out=out[g, half * M_TILE : (half + 1) * M_TILE, :], in_=res[:])
+        halves = range(M // M_TILE)
+        z_banks = [product(w_codes, w_scales, half, "z") for half in halves]
+        v_banks = [product(u_codes, u_scales, half, "v") for half in halves]
+        blocks = [(half, g) for half in halves for g in range(G)]
+        for half, g in blocks:
+            gate = sb.tile([M_TILE, N], F32, name="gate_%d_%d" % (half, g), align_bytes=64)
+            nc.scalar.activation(out=gate[:], in_=z_banks[half][g][:], func=SIGMOID)
+            res = sb.tile([M_TILE, N], F32, name="res_%d_%d" % (half, g), align_bytes=64)
+            width = N // 2 if (half, g) == blocks[-1] else N
+            for n0 in range(0, N, width):
+                cols = slice(n0, n0 + width)
+                nc.vector.tensor_tensor(
+                    out=res[:, cols], in0=v_banks[half][g][:, cols], in1=gate[:, cols], op=mybir.AluOpType.mult
+                )
+                nc.sync.dma_start(out=out[g, half * M_TILE : (half + 1) * M_TILE, cols], in_=res[:, cols])

from contextlib import ExitStack

import concourse.mybir as mybir

G, D, M, N = 2, 256, 256, 512
FLOPS = 2 * 2 * G * D * M * N

F32 = mybir.dt.float32
BF16 = mybir.dt.bfloat16
U32 = mybir.dt.uint32
U8 = mybir.dt.uint8
FP8X4 = mybir.dt.float8_e4m3fn_x4
SIGMOID = mybir.ActivationFunctionType.Sigmoid

P = 128
PACK = 4
ROWS = D // PACK
M_TILE = 128
RUN = 4
X_HALF = N // 2
X_VECTOR_COLS = 288
W_VECTOR_COLS = 64
U_VECTOR_COLS = 80


def interleave(copy, grouped, raw, c0, c1):
    copy(
        out=grouped[:, c0 * PACK : c1 * PACK].rearrange("p (c i j) -> p c j i", i=RUN, j=PACK),
        in_=raw[:, :, c0:c1].rearrange("p j (c i) -> p c j i", i=RUN),
    )


def quantize(nc, codes, scales, grouped, c0, c1):
    nc.vector.quantize_mx(
        out=codes[:, c0:c1].bitcast(FP8X4),
        scales=scales[:, c0:c1],
        in_=grouped[:, c0 * PACK : c1 * PACK],
    )


def tile_rows_gglu_sigmoid_kernel(tc, x, w, u, out):
    nc = tc.nc
    with ExitStack() as ctx:
        sb = ctx.enter_context(tc.tile_pool(name="sb", bufs=1))
        ps = ctx.enter_context(tc.psum_pool(name="ps", bufs=1))
        ctx.enter_context(tc.manual_schedule())

        x_raw = sb.tile([P, PACK, N], F32, name="x_raw", align_bytes=64)
        w_raw = sb.tile([P, PACK, M], F32, name="w_raw", align_bytes=64)
        u_raw = sb.tile([P, PACK, M], F32, name="u_raw", align_bytes=64)
        for raw, src in ((x_raw, x), (w_raw, w), (u_raw, u)):
            nc.sync.dma_start(out=raw[:], in_=src.rearrange("g (p j) c -> (g p) j c", j=PACK))

        warm_in = sb.tile([P, 1], F32, name="warm_in")
        warm_out = sb.tile([P, 1], F32, name="warm_out")
        nc.gpsimd.memset(warm_in[:], 0.0)
        nc.scalar.activation(out=warm_out[:], in_=warm_in[:], func=SIGMOID)

        x_bf = sb.tile([P, N * PACK], BF16, name="x_bf", align_bytes=64)
        x_codes = sb.tile([P, N], U32, name="x_codes", align_bytes=64)
        x_scales = sb.tile([P, N], U8, name="x_scales", align_bytes=64)
        w_bf = sb.tile([P, M * PACK], BF16, name="w_bf", align_bytes=64)
        w_codes = sb.tile([P, M], U32, name="w_codes", align_bytes=64)
        w_scales = sb.tile([P, M], U8, name="w_scales", align_bytes=64)
        u_bf = sb.tile([P, M * PACK], BF16, name="u_bf", align_bytes=64)
        u_codes = sb.tile([P, M], U32, name="u_codes", align_bytes=64)
        u_scales = sb.tile([P, M], U8, name="u_scales", align_bytes=64)

        def product(codes, scales, half, label):
            banks = []
            cols = slice(half * M_TILE, (half + 1) * M_TILE)
            for g in range(G):
                rows = slice(g * ROWS, (g + 1) * ROWS)
                bank = ps.tile([M_TILE, N], F32, name="%s_%d_%d" % (label, half, g))
                nc.tensor.matmul_mx(
                    out=bank[:],
                    lhsT=codes[rows, cols].bitcast(FP8X4),
                    lhsT_scale=scales[rows, cols],
                    rhs=x_codes[rows, :].bitcast(FP8X4),
                    rhs_scale=x_scales[rows, :],
                    start=True,
                    stop=True,
                )
                banks.append(bank)
            return banks

        vcopy, scopy = nc.vector.tensor_copy, nc.scalar.copy
        interleave(vcopy, x_bf, x_raw, 0, X_HALF)
        interleave(vcopy, x_bf, x_raw, X_HALF, X_VECTOR_COLS)
        interleave(scopy, x_bf, x_raw, X_VECTOR_COLS, N)
        quantize(nc, x_codes, x_scales, x_bf, 0, X_HALF)
        interleave(vcopy, w_bf, w_raw, 0, W_VECTOR_COLS)
        interleave(scopy, w_bf, w_raw, W_VECTOR_COLS, M_TILE)
        interleave(scopy, w_bf, w_raw, M_TILE, M)
        quantize(nc, x_codes, x_scales, x_bf, X_HALF, N)
        quantize(nc, w_codes, w_scales, w_bf, 0, M_TILE)
        quantize(nc, w_codes, w_scales, w_bf, M_TILE, M)
        for m0 in range(0, M, M_TILE):
            interleave(vcopy, u_bf, u_raw, m0, m0 + U_VECTOR_COLS)
            interleave(scopy, u_bf, u_raw, m0 + U_VECTOR_COLS, m0 + M_TILE)
        quantize(nc, u_codes, u_scales, u_bf, 0, M_TILE)
        quantize(nc, u_codes, u_scales, u_bf, M_TILE, M)

        halves = range(M // M_TILE)
        z_banks = [product(w_codes, w_scales, half, "z") for half in halves]
        v_banks = [product(u_codes, u_scales, half, "v") for half in halves]
        blocks = [(half, g) for half in halves for g in range(G)]
        for half, g in blocks:
            gate = sb.tile([M_TILE, N], F32, name="gate_%d_%d" % (half, g), align_bytes=64)
            nc.scalar.activation(out=gate[:], in_=z_banks[half][g][:], func=SIGMOID)
            res = sb.tile([M_TILE, N], F32, name="res_%d_%d" % (half, g), align_bytes=64)
            width = N // 2 if (half, g) == blocks[-1] else N
            for n0 in range(0, N, width):
                cols = slice(n0, n0 + width)
                nc.vector.tensor_tensor(
                    out=res[:, cols], in0=v_banks[half][g][:, cols], in1=gate[:, cols], op=mybir.AluOpType.mult
                )
                nc.sync.dma_start(out=out[g, half * M_TILE : (half + 1) * M_TILE, cols], in_=res[:, cols])
